import numpy as np
import ml_dtypes


def mxq(x, axis, fmt="e4m3"):
    dtype, down = {"e4m3": (ml_dtypes.float8_e4m3fn, 7), "e5m2": (ml_dtypes.float8_e5m2, 14)}[fmt]
    v = np.moveaxis(np.asarray(x, np.float32).astype(ml_dtypes.bfloat16).astype(np.float64), axis, -1)
    blocks = v.reshape(v.shape[:-1] + (-1, 32))
    amax = np.abs(blocks).max(-1, keepdims=True)
    byte = np.maximum(np.where(amax > 0, np.frexp(amax)[1] - 1 + 127, 0) - down, 1)
    scale = np.exp2(byte - 127.0)
    codes = (blocks / scale).astype(np.float32).astype(dtype).astype(np.float64)
    return np.moveaxis((codes * scale).reshape(v.shape), -1, axis)


WIDE = False


def mx_kscale(k):
    if not WIDE:
        return np.ones(k)
    levels = np.array([10, -10, 5, -5, 0])
    if k % 512:
        return np.exp2(np.random.permutation(np.resize(levels, k // 32))).repeat(32)
    a = np.empty((k // 512, 16))
    for p in range(k // 512):
        a[p, :8] = np.random.permutation(np.resize(levels, 8))
        for g in range(8):
            far = levels[np.abs(levels - a[p, g]) >= 10]
            a[p, g + 8] = far[np.random.randint(len(far))]
    return np.exp2(a.ravel()).repeat(32)


def f64(x):
    return np.asarray(x).astype(np.float64)


def striped(idx):
    return np.tile(np.asarray(idx).reshape(-1, 16).T, (8, 1)).astype(np.uint16)


def unstriped(offs):
    return offs[:16].T.reshape(-1).astype(np.int64)


E2M1 = np.array([0.0, 0.5, 1.0, 1.5, 2.0, 3.0, 4.0, 6.0, -0.0, -0.5, -1.0, -1.5, -2.0, -3.0, -4.0, -6.0])


def pack_weight(w, fmt):
    k, n = w.shape
    w = f64(np.asarray(w, np.float32).astype(ml_dtypes.bfloat16)).reshape(k // 32, 32, n)
    amax = np.abs(w).max(1)
    if fmt == "e4m3":
        byte = np.frexp(amax)[1] - 1 + 127 - 7
    else:
        mant, ex = np.frexp(amax / 6.0)
        byte = np.where(mant > 0.5, ex, ex - 1) + 127
    byte = np.clip(np.where(amax > 0, byte, 1), 1, 254)
    scaled = (w * np.exp2(127.0 - byte)[:, None, :]).reshape(k, n).astype(np.float32)
    by_word = np.ascontiguousarray(scaled.reshape(k // 512, 128, 4, n).transpose(0, 1, 3, 2))
    if fmt == "e4m3":
        words = by_word.astype(ml_dtypes.float8_e4m3fn).view(np.uint8)
    else:
        c = by_word.astype(ml_dtypes.float4_e2m1fn).view(np.uint8) & 0xF
        words = (c[..., 0::2] | (c[..., 1::2] << 4)).reshape(k // 512, 128, 2 * n)
    return np.ascontiguousarray(words), np.ascontiguousarray(byte.astype(np.uint8).reshape(k // 512, 16, n))


def unpack_weight(words, scales, fmt):
    g, _, n = scales.shape
    words = np.ascontiguousarray(words).reshape(g, 128, n, -1)
    if fmt == "e4m3":
        vals = words.view(ml_dtypes.float8_e4m3fn).astype(np.float64)
    else:
        nib = np.empty((g, 128, n, 4), np.uint8)
        nib[..., 0::2] = words & 0xF
        nib[..., 1::2] = words >> 4
        vals = E2M1[nib]
    vals = vals * np.repeat(np.exp2(scales.astype(np.float64) - 127.0), 8, axis=1)[..., None]
    return vals.transpose(0, 1, 3, 2).reshape(g * 512, n)


D, K, E, T, I, Q = 512, 1024, 512, 1024, 256, 128


def setup_inputs():
    n = np.random.standard_normal
    idx = np.random.permutation(T)[:I]
    fd = mx_kscale(D)
    fk = mx_kscale(K)
    fe = mx_kscale(E)
    fkeysp = pack_weight(n((K, T)) / fk[:, None], "e4m3")
    return {
        "query": (n((D, Q)) * 0.4 / np.sqrt(D) * fd[:, None]).astype(np.float32),
        "fquery": (n((K, Q)) * 1.2 / np.sqrt(K) * fk[:, None]).astype(np.float32),
        "ckeys": (n((D, T)) / fd[:, None]).astype(np.float32),
        "fkeys_words": fkeysp[0],
        "fkeys_scales": fkeysp[1],
        "share": (np.random.uniform(0.3, 0.9, (Q, 1))).astype(np.float32),
        "gout": (n((E, Q)) * 1 / np.sqrt(E) * fe[:, None]).astype(np.float32),
        "vals": (n((E, T)) / fe[:, None]).astype(np.float32),
        "fac": (np.random.uniform(0.5, 2.0, (1, T))).astype(np.float32),
        "dfquery": (n((K, Q)) * 1.0 / np.sqrt(K) * fk[:, None]).astype(np.float32),
        "base": (0.5 * n((Q, I))).astype(np.float32),
        "offs": striped(idx),
    }


def reference(query, fquery, ckeys, fkeys_words, fkeys_scales, share, gout, vals, fac, dfquery, base, offs):
    idx = unstriped(offs)
    fkeysu = unpack_weight(fkeys_words, fkeys_scales, "e4m3")
    queryq = mxq(f64(query), 0, "e4m3")
    ckeysq = mxq(f64(ckeys), 0, "e4m3")
    a = queryq.T @ ckeysq
    fqueryq = mxq(f64(fquery), 0, "e4m3")
    fkeysidxg = fkeysu[:, idx]
    b = fqueryq.T @ fkeysidxg
    dfqueryq = mxq(f64(dfquery), 0, "e4m3")
    tb = dfqueryq.T @ fkeysidxg
    dl = (b - a[:, idx]) * f64(share)
    df1 = np.zeros((Q, T))
    df1[:, idx] = dl
    s = a + df1
    p = np.exp(s - np.max(s, axis=1, keepdims=True))
    z = np.sum(p, axis=1, keepdims=True)
    goutq = mxq(f64(gout), 0, "e4m3")
    valsq = mxq(f64(vals), 0, "e4m3")
    c0 = goutq.T @ valsq
    dz = np.sum(c0 * p * f64(fac) / np.square(z) * (-1.0), axis=1, keepdims=True)
    dp = c0 / z * f64(fac) + dz
    xdl = tb * f64(share)
    xdf1 = np.zeros((Q, T))
    xdf1[:, idx] = xdl
    xs = xdf1
    xp = xs * p
    xz = np.sum(xp, axis=1, keepdims=True)
    xdz = np.sum((xp * f64(fac) * c0 - xz * z * 2.0 * c0 * p * f64(fac) / np.square(z)) / np.square(z) * (-1.0), axis=1, keepdims=True)
    xdp = xz * c0 / np.square(z) * (-1.0) * f64(fac) + xdz
    xds = xdp * p + xp * dp
    xddl = xds[:, idx]
    xdb = xddl * f64(share)
    y = xdb * 1024.0 + f64(base)
    return y

@@ -1,0 +1,209 @@
+from contextlib import ExitStack
+
+import concourse.mybir as mybir
+from concourse.masks import make_identity
+
+D, K, E, T, I, Q = 512, 1024, 512, 1024, 256, 128
+FLOPS = 2 * Q * (D * T + 2 * K * I + E * T)
+
+F32 = mybir.dt.float32
+BF16 = mybir.dt.bfloat16
+I32 = mybir.dt.int32
+U32 = mybir.dt.uint32
+U16 = mybir.dt.uint16
+U8 = mybir.dt.uint8
+FP8X4 = mybir.dt.float8_e4m3fn_x4
+ALU = mybir.AluOpType
+ACT = mybir.ActivationFunctionType
+
+P = 128
+PACK = 4
+CHUNK = 256
+BANK = 512
+LAST_ON_VECTOR = 160
+
+
+def tile_attend_hvrefined_b_kernel(tc, query, fquery, ckeys, fkeys_words, fkeys_scales, share, gout, vals, fac, dfquery, base, offs, out):
+    nc = tc.nc
+    with ExitStack() as ctx:
+        sb = ctx.enter_context(tc.tile_pool(name="sb", bufs=1))
+        ps = ctx.enter_context(tc.psum_pool(name="ps", bufs=1))
+
+        def load_rows(name, rows, split=False):
+            passes, width = rows.shape[0] // (P * PACK), rows.shape[1]
+            raw = sb.tile([P, passes, PACK, width], F32, name=name + "_raw", tag=name + "_raw")
+            by_pass = rows.rearrange("(g p j) w -> g p j w", p=P, j=PACK)
+            if split:
+                for g in range(passes):
+                    nc.sync.dma_start(out=raw[:, g], in_=by_pass[g])
+            else:
+                nc.sync.dma_start(out=raw[:], in_=by_pass.rearrange("g p j w -> p g j w"))
+            return raw
+
+        def interleave(on_vector, grouped, raw):
+            dst = grouped.rearrange("p (c i) t -> p c t i", i=4)
+            src = raw.rearrange("p t (c i) -> p c t i", i=4)
+            if on_vector:
+                nc.vector.tensor_copy(out=dst, in_=src)
+            else:
+                nc.scalar.activation(out=dst, in_=src, func=ACT.Copy)
+
+        def quantize(name, raw, vector_columns):
+            passes, width = raw.shape[1], raw.shape[3]
+            grouped = sb.tile([P, passes, width, PACK], BF16, name=name + "_grouped", align_bytes=64)
+            for g in range(passes):
+                if vector_columns < width:
+                    interleave(False, grouped[:, g, vector_columns:, :], raw[:, g, :, vector_columns:])
+                if vector_columns > 0:
+                    interleave(True, grouped[:, g, :vector_columns, :], raw[:, g, :, :vector_columns])
+            codes = sb.tile([P, passes * width], U32, name=name + "_codes", align_bytes=64)
+            scales = sb.tile([P, passes * width], U8, name=name + "_scales", align_bytes=64)
+            nc.vector.quantize_mx(out=codes[:].bitcast(FP8X4), scales=scales[:], in_=grouped[:].rearrange("p g w t -> p (g w t)"))
+            return codes, scales
+
+        def column(name):
+            return sb.tile([P, 1], F32, name=name)
+
+        key_scales = sb.tile([P, T], U8, name="key_scales")
+        nc.gpsimd.memset(key_scales[:].bitcast(I32), 0)
+        identity = sb.tile([P, P], F32, name="identity")
+        make_identity(nc, identity[:])
+
+        fac_cols = sb.tile([P, T // P], F32, name="fac_cols")
+        nc.sync.dma_start(out=fac_cols[:], in_=fac.rearrange("o (p c) -> p (o c)", p=P))
+        offsets = sb.tile([P, I // 16], U16, name="offsets")
+        nc.sync.dma_start(offsets[:], offs)
+        share_col = column("share_col")
+        nc.sync.dma_start(out=share_col[:], in_=share)
+        dfq_raw = load_rows("dfq", dfquery, True)
+        for quad in range(4):
+            nc.sync.dma_start(out=key_scales[32 * quad : 32 * quad + 8, :].bitcast(I32), in_=fkeys_scales[:, 4 * quad : 4 * quad + 4, :].bitcast(I32))
+        key_words = []
+        for g in range(2):
+            words = sb.tile([P, T], I32, name="key_words%d" % g)
+            source = fkeys_words[g].rearrange("p n t -> p (n t)").bitcast(I32)
+            for piece in range(g + 1):
+                cols = slice(piece * T // (g + 1), (piece + 1) * T // (g + 1))
+                nc.sync.dma_start(out=words[:, cols], in_=source[:, cols])
+            key_words.append(words)
+        fq_raw = load_rows("fq", fquery)
+        q_raw = load_rows("q", query)
+        ck_raw = [load_rows("ck%d" % c, ckeys[:, c * CHUNK : (c + 1) * CHUNK]) for c in range(T // CHUNK)]
+        gout_raw = load_rows("gout", gout)
+        val_raw = [load_rows("val%d" % c, vals[:, c * CHUNK : (c + 1) * CHUNK]) for c in range(T // CHUNK)]
+        base_sb = sb.tile([P, I], F32, name="base_sb")
+        nc.sync.dma_start(out=base_sb[:], in_=base)
+
+        xs = sb.tile([P, T], F32, name="xs")
+        nc.vector.memset(xs[:], 0.0)
+        df1 = sb.tile([P, T], F32, name="df1")
+        nc.vector.memset(df1[:], 0.0)
+
+        fac_rows = sb.tile([P, T], F32, name="fac_rows")
+        for h in range(2):
+            bank = ps.tile([P, 4, P], F32, name="fac_bank%d" % h, tag="late%d" % h)
+            for c in range(4):
+                nc.tensor.transpose(bank[:, c, :], fac_cols[:, 4 * h + c : 4 * h + c + 1].to_broadcast([P, P]), identity[:])
+            nc.vector.tensor_copy(out=fac_rows[:].rearrange("p (n e) -> p n e", e=8)[:, :, 4 * h : 4 * h + 4], in_=bank[:].rearrange("p c n -> p n c"))
+        neg_share = sb.tile([P, I], F32, name="neg_share")
+        nc.vector.tensor_scalar(out=neg_share[:], in0=share_col[:].to_broadcast([P, I]), scalar1=-1.0, scalar2=None, op0=ALU.mult)
+        rest = column("rest")
+        nc.vector.tensor_scalar(out=rest[:], in0=share_col[:], scalar1=-1.0, scalar2=1.0, op0=ALU.mult, op1=ALU.add)
+        out_scale = column("out_scale")
+        nc.vector.tensor_scalar(out=out_scale[:], in0=share_col[:], scalar1=1024.0, scalar2=None, op0=ALU.mult)
+
+        dfq_codes, dfq_scales = quantize("dfq", dfq_raw, 0)
+        picked_words = []
+        for g in range(2):
+            picked = sb.tile([P, I], U32, name="picked_words%d" % g, align_bytes=64)
+            nc.vector.tensor_copy(picked[:], key_words[g][:].bitcast(U32).indirect(offsets[:]))
+            picked_words.append(picked)
+        picked_scales = sb.tile([P, I], U8, name="picked_scales", align_bytes=64)
+        nc.vector.tensor_copy(picked_scales[:], key_scales[:].indirect(offsets[:]))
+
+        def fine_product(acc, codes, scales):
+            for g in range(2):
+                nc.tensor.matmul_mx(
+                    out=acc,
+                    lhsT=codes[:, g * Q : (g + 1) * Q].bitcast(FP8X4),
+                    lhsT_scale=scales[:, g * Q : (g + 1) * Q],
+                    rhs=picked_words[g][:].bitcast(FP8X4),
+                    rhs_scale=picked_scales[4 * g :, :],
+                    start=(g == 0),
+                    stop=(g == 1),
+                )
+
+        tb_bank = ps.tile([P, I], F32, name="tb_bank")
+        fine_product(tb_bank[:], dfq_codes, dfq_scales)
+        xdl = sb.tile([P, I], F32, name="xdl")
+        nc.vector.tensor_scalar(out=xdl[:], in0=tb_bank[:], scalar1=share_col[:], scalar2=None, op0=ALU.mult)
+        nc.vector.tensor_copy(xs[:].indirect(offsets[:]), xdl[:])
+
+        fq_codes, fq_scales = quantize("fq", fq_raw, 0)
+        b_bank = ps.tile([P, I], F32, name="b_bank")
+        fine_product(b_bank[:], fq_codes, fq_scales)
+        b_sb = sb.tile([P, I], F32, name="b_sb")
+        nc.vector.tensor_copy(out=b_sb[:], in_=b_bank[:])
+
+        q_codes, q_scales = quantize("q", q_raw, 0)
+        ck_on_vector = [0, CHUNK, 0, LAST_ON_VECTOR]
+        a_banks = [ps.tile([P, BANK], F32, name="a_bank01"), ps.tile([P, CHUNK], F32, name="a_bank2"), ps.tile([P, CHUNK], F32, name="a_bank3")]
+        a_out = [a_banks[0][:, :CHUNK], a_banks[0][:, CHUNK:], a_banks[1][:], a_banks[2][:]]
+        for c in range(T // CHUNK):
+            codes, scales = quantize("ck%d" % c, ck_raw[c], ck_on_vector[c])
+            nc.tensor.matmul_mx(out=a_out[c], lhsT=q_codes[:].bitcast(FP8X4), lhsT_scale=q_scales[:], rhs=codes[:].bitcast(FP8X4), rhs_scale=scales[:], start=True, stop=True)
+        a_sb = sb.tile([P, T], F32, name="a_sb", tag="ck3_raw")
+        nc.scalar.copy(out=a_sb[:, :BANK], in_=a_banks[0][:])
+        nc.scalar.copy(out=a_sb[:, BANK : BANK + CHUNK], in_=a_banks[1][:])
+        nc.vector.tensor_copy(out=a_sb[:, BANK + CHUNK :], in_=a_banks[2][:])
+
+        gap = sb.tile([P, I], F32, name="gap")
+        nc.vector.tensor_tensor(gap[:], a_sb[:].indirect(offsets[:]), b_sb[:], ALU.subtract)
+        nc.vector.tensor_tensor(df1[:].indirect(offsets[:]), gap[:], neg_share[:], ALU.mult)
+        s = sb.tile([P, T], F32, name="s")
+        nc.vector.tensor_tensor(s[:], a_sb[:], df1[:], ALU.add)
+        neg_max = column("neg_max")
+        nc.vector.tensor_reduce(out=neg_max[:], in_=s[:], axis=mybir.AxisListType.X, op=ALU.max, negate=True)
+
+        gout_codes, gout_scales = quantize("gout", gout_raw, 0)
+        val_q = [quantize("val%d" % c, val_raw[c], 0) for c in range(T // CHUNK)]
+
+        p = sb.tile([P, T], F32, name="p", tag="val3_raw")
+        z = column("z")
+        nc.scalar.activation(out=p[:], in_=s[:], func=ACT.Exp, bias=neg_max[:], accum_out=z[:])
+        s_listed = sb.tile([P, I], F32, name="s_listed")
+        nc.vector.scalar_tensor_tensor(out=s_listed[:], in0=gap[:], scalar=rest[:], in1=b_sb[:], op0=ALU.mult, op1=ALU.add)
+        p_listed = sb.tile([P, I], F32, name="p_listed")
+        nc.scalar.activation(out=p_listed[:], in_=s_listed[:], func=ACT.Exp, bias=neg_max[:])
+
+        neg_g = sb.tile([P, T], F32, name="neg_g")
+        for h in range(2):
+            bank = ps.tile([P, BANK], F32, name="c0_bank%d" % h, tag="late%d" % h)
+            for c in range(2):
+                codes, scales = val_q[2 * h + c]
+                nc.tensor.matmul_mx(out=bank[:, c * CHUNK : (c + 1) * CHUNK], lhsT=gout_codes[:].bitcast(FP8X4), lhsT_scale=gout_scales[:], rhs=codes[:].bitcast(FP8X4), rhs_scale=scales[:], start=True, stop=True)
+            nc.vector.scalar_tensor_tensor(out=neg_g[:, h * BANK : (h + 1) * BANK], in0=bank[:], scalar=-1.0, in1=fac_rows[:, h * BANK : (h + 1) * BANK], op0=ALU.mult, op1=ALU.mult)
+
+        inv_z = column("inv_z")
+        nc.vector.reciprocal(out=inv_z[:], in_=z[:])
+        prob = sb.tile([P, T], F32, name="prob")
+        nc.scalar.activation(out=prob[:], in_=p[:], func=ACT.Copy, scale=inv_z[:])
+
+        spent = sb.tile([P, T], F32, name="spent")
+        neg_mean_g = column("neg_mean_g")
+        nc.vector.scalar_tensor_tensor(out=spent[:], in0=p[:], scalar=inv_z[:], in1=neg_g[:], op0=ALU.mult, op1=ALU.mult, accum_out=neg_mean_g[:])
+        spent_listed = sb.tile([P, I], F32, name="spent_listed")
+        mean_xs = column("mean_xs")
+        nc.vector.scalar_tensor_tensor(out=spent_listed[:], in0=p_listed[:], scalar=inv_z[:], in1=xdl[:], op0=ALU.mult, op1=ALU.mult, accum_out=mean_xs[:])
+        neg_v = sb.tile([P, T], F32, name="neg_v")
+        nc.vector.scalar_tensor_tensor(out=neg_v[:], in0=neg_g[:], scalar=neg_mean_g[:], in1=prob[:], op0=ALU.subtract, op1=ALU.mult)
+        neg_y = sb.tile([P, T], F32, name="neg_y")
+        neg_cov = column("neg_cov")
+        nc.vector.scalar_tensor_tensor(out=neg_y[:], in0=xs[:], scalar=mean_xs[:], in1=neg_v[:], op0=ALU.subtract, op1=ALU.mult, accum_out=neg_cov[:])
+        xds = sb.tile([P, T], F32, name="xds")
+        nc.vector.scalar_tensor_tensor(out=xds[:], in0=prob[:], scalar=neg_cov[:], in1=neg_y[:], op0=ALU.mult, op1=ALU.subtract)
+        xddl = sb.tile([P, I], F32, name="xddl")
+        nc.vector.tensor_copy(xddl[:], xds[:].indirect(offsets[:]))
+        result = sb.tile([P, I], F32, name="result")
+        nc.vector.scalar_tensor_tensor(out=result[:], in0=xddl[:], scalar=out_scale[:], in1=base_sb[:], op0=ALU.mult, op1=ALU.add)
+        nc.sync.dma_start(out=out, in_=result[:])

@@ -29,15 +29,10 @@ def tile_attend_hvrefined_b_kernel(tc, query, fquery, ckeys, fkeys_words, fkeys_
         sb = ctx.enter_context(tc.tile_pool(name="sb", bufs=1))
         ps = ctx.enter_context(tc.psum_pool(name="ps", bufs=1))
 
-        def load_rows(name, rows, split=False):
+        def load_rows(name, rows):
             passes, width = rows.shape[0] // (P * PACK), rows.shape[1]
             raw = sb.tile([P, passes, PACK, width], F32, name=name + "_raw", tag=name + "_raw")
-            by_pass = rows.rearrange("(g p j) w -> g p j w", p=P, j=PACK)
-            if split:
-                for g in range(passes):
-                    nc.sync.dma_start(out=raw[:, g], in_=by_pass[g])
-            else:
-                nc.sync.dma_start(out=raw[:], in_=by_pass.rearrange("g p j w -> p g j w"))
+            nc.sync.dma_start(out=raw[:], in_=rows.rearrange("(g p j) w -> p g j w", p=P, j=PACK))
             return raw
 
         def interleave(on_vector, grouped, raw):
@@ -50,7 +45,7 @@ def tile_attend_hvrefined_b_kernel(tc, query, fquery, ckeys, fkeys_words, fkeys_
 
         def quantize(name, raw, vector_columns):
             passes, width = raw.shape[1], raw.shape[3]
-            grouped = sb.tile([P, passes, width, PACK], BF16, name=name + "_grouped", align_bytes=64)
+            grouped = sb.tile([P, passes, width, PACK], BF16, name=name + "_grouped", tag=name + "_grouped", align_bytes=64)
             for g in range(passes):
                 if vector_columns < width:
                     interleave(False, grouped[:, g, vector_columns:, :], raw[:, g, :, vector_columns:])
@@ -73,22 +68,22 @@ def tile_attend_hvrefined_b_kernel(tc, query, fquery, ckeys, fkeys_words, fkeys_
         nc.sync.dma_start(out=fac_cols[:], in_=fac.rearrange("o (p c) -> p (o c)", p=P))
         offsets = sb.tile([P, I // 16], U16, name="offsets")
         nc.sync.dma_start(offsets[:], offs)
-        share_col = column("share_col")
-        nc.sync.dma_start(out=share_col[:], in_=share)
-        dfq_raw = load_rows("dfq", dfquery, True)
+
+        def load_words(g):
+            words = sb.tile([P, T], I32, name="key_words%d" % g)
+            nc.sync.dma_start(out=words[:], in_=fkeys_words[g].rearrange("p n t -> p (n t)").bitcast(I32))
+            return words
+
+        dfq_raw = load_rows("dfq", dfquery)
+        key_words = [load_words(0)]
         for quad in range(4):
             nc.sync.dma_start(out=key_scales[32 * quad : 32 * quad + 8, :].bitcast(I32), in_=fkeys_scales[:, 4 * quad : 4 * quad + 4, :].bitcast(I32))
-        key_words = []
-        for g in range(2):
-            words = sb.tile([P, T], I32, name="key_words%d" % g)
-            source = fkeys_words[g].rearrange("p n t -> p (n t)").bitcast(I32)
-            for piece in range(g + 1):
-                cols = slice(piece * T // (g + 1), (piece + 1) * T // (g + 1))
-                nc.sync.dma_start(out=words[:, cols], in_=source[:, cols])
-            key_words.append(words)
-        fq_raw = load_rows("fq", fquery)
+        key_words.append(load_words(1))
+        share_col = column("share_col")
+        nc.sync.dma_start(out=share_col[:], in_=share)
         q_raw = load_rows("q", query)
         ck_raw = [load_rows("ck%d" % c, ckeys[:, c * CHUNK : (c + 1) * CHUNK]) for c in range(T // CHUNK)]
+        fq_raw = [load_rows("fq%d" % g, fquery[g * P * PACK : (g + 1) * P * PACK, :]) for g in range(2)]
         gout_raw = load_rows("gout", gout)
         val_raw = [load_rows("val%d" % c, vals[:, c * CHUNK : (c + 1) * CHUNK]) for c in range(T // CHUNK)]
         base_sb = sb.tile([P, I], F32, name="base_sb")
@@ -104,11 +99,9 @@ def tile_attend_hvrefined_b_kernel(tc, query, fquery, ckeys, fkeys_words, fkeys_
             bank = ps.tile([P, 4, P], F32, name="fac_bank%d" % h, tag="late%d" % h)
             for c in range(4):
                 nc.tensor.transpose(bank[:, c, :], fac_cols[:, 4 * h + c : 4 * h + c + 1].to_broadcast([P, P]), identity[:])
-            nc.vector.tensor_copy(out=fac_rows[:].rearrange("p (n e) -> p n e", e=8)[:, :, 4 * h : 4 * h + 4], in_=bank[:].rearrange("p c n -> p n c"))
+            nc.scalar.copy(out=fac_rows[:].rearrange("p (n e) -> p n e", e=8)[:, :, 4 * h : 4 * h + 4], in_=bank[:].rearrange("p c n -> p n c"))
         neg_share = sb.tile([P, I], F32, name="neg_share")
         nc.vector.tensor_scalar(out=neg_share[:], in0=share_col[:].to_broadcast([P, I]), scalar1=-1.0, scalar2=None, op0=ALU.mult)
-        rest = column("rest")
-        nc.vector.tensor_scalar(out=rest[:], in0=share_col[:], scalar1=-1.0, scalar2=1.0, op0=ALU.mult, op1=ALU.add)
         out_scale = column("out_scale")
         nc.vector.tensor_scalar(out=out_scale[:], in0=share_col[:], scalar1=1024.0, scalar2=None, op0=ALU.mult)
 
@@ -121,68 +114,68 @@ def tile_attend_hvrefined_b_kernel(tc, query, fquery, ckeys, fkeys_words, fkeys_
         picked_scales = sb.tile([P, I], U8, name="picked_scales", align_bytes=64)
         nc.vector.tensor_copy(picked_scales[:], key_scales[:].indirect(offsets[:]))
 
-        def fine_product(acc, codes, scales):
-            for g in range(2):
+        def fine_product(acc, by_pass):
+            for g, (codes, scales) in enumerate(by_pass):
                 nc.tensor.matmul_mx(
                     out=acc,
-                    lhsT=codes[:, g * Q : (g + 1) * Q].bitcast(FP8X4),
-                    lhsT_scale=scales[:, g * Q : (g + 1) * Q],
+                    lhsT=codes.bitcast(FP8X4),
+                    lhsT_scale=scales,
                     rhs=picked_words[g][:].bitcast(FP8X4),
                     rhs_scale=picked_scales[4 * g :, :],
                     start=(g == 0),
                     stop=(g == 1),
                 )
 
-        tb_bank = ps.tile([P, I], F32, name="tb_bank")
-        fine_product(tb_bank[:], dfq_codes, dfq_scales)
+        q_codes, q_scales = quantize("q", q_raw, Q)
+        tb_bank = ps.tile([P, I], F32, name="tb_bank", tag="late1")
+        fine_product(tb_bank[:], [(dfq_codes[:, g * Q : (g + 1) * Q], dfq_scales[:, g * Q : (g + 1) * Q]) for g in range(2)])
         xdl = sb.tile([P, I], F32, name="xdl")
         nc.vector.tensor_scalar(out=xdl[:], in0=tb_bank[:], scalar1=share_col[:], scalar2=None, op0=ALU.mult)
         nc.vector.tensor_copy(xs[:].indirect(offsets[:]), xdl[:])
 
-        fq_codes, fq_scales = quantize("fq", fq_raw, 0)
-        b_bank = ps.tile([P, I], F32, name="b_bank")
-        fine_product(b_bank[:], fq_codes, fq_scales)
-        b_sb = sb.tile([P, I], F32, name="b_sb")
-        nc.vector.tensor_copy(out=b_sb[:], in_=b_bank[:])
-
-        q_codes, q_scales = quantize("q", q_raw, 0)
-        ck_on_vector = [0, CHUNK, 0, LAST_ON_VECTOR]
+        ck_on_vector = [0, 0, 0, LAST_ON_VECTOR]
         a_banks = [ps.tile([P, BANK], F32, name="a_bank01"), ps.tile([P, CHUNK], F32, name="a_bank2"), ps.tile([P, CHUNK], F32, name="a_bank3")]
         a_out = [a_banks[0][:, :CHUNK], a_banks[0][:, CHUNK:], a_banks[1][:], a_banks[2][:]]
         for c in range(T // CHUNK):
             codes, scales = quantize("ck%d" % c, ck_raw[c], ck_on_vector[c])
             nc.tensor.matmul_mx(out=a_out[c], lhsT=q_codes[:].bitcast(FP8X4), lhsT_scale=q_scales[:], rhs=codes[:].bitcast(FP8X4), rhs_scale=scales[:], start=True, stop=True)
-        a_sb = sb.tile([P, T], F32, name="a_sb", tag="ck3_raw")
+        fq = [quantize("fq%d" % g, fq_raw[g], g * Q) for g in range(2)]
+        b_bank = ps.tile([P, I], F32, name="b_bank")
+        fine_product(b_bank[:], [(codes[:], scales[:]) for codes, scales in fq])
+        a_sb = sb.tile([P, T], F32, name="a_sb", tag="fq0_raw")
         nc.scalar.copy(out=a_sb[:, :BANK], in_=a_banks[0][:])
         nc.scalar.copy(out=a_sb[:, BANK : BANK + CHUNK], in_=a_banks[1][:])
         nc.vector.tensor_copy(out=a_sb[:, BANK + CHUNK :], in_=a_banks[2][:])
 
+        a_listed = sb.tile([P, I], F32, name="a_listed")
+        nc.vector.tensor_copy(a_listed[:], a_sb[:].indirect(offsets[:]))
         gap = sb.tile([P, I], F32, name="gap")
-        nc.vector.tensor_tensor(gap[:], a_sb[:].indirect(offsets[:]), b_sb[:], ALU.subtract)
+        nc.vector.tensor_tensor(gap[:], a_listed[:], b_bank[:], ALU.subtract)
         nc.vector.tensor_tensor(df1[:].indirect(offsets[:]), gap[:], neg_share[:], ALU.mult)
         s = sb.tile([P, T], F32, name="s")
         nc.vector.tensor_tensor(s[:], a_sb[:], df1[:], ALU.add)
-        neg_max = column("neg_max")
-        nc.vector.tensor_reduce(out=neg_max[:], in_=s[:], axis=mybir.AxisListType.X, op=ALU.max, negate=True)
-
         gout_codes, gout_scales = quantize("gout", gout_raw, 0)
-        val_q = [quantize("val%d" % c, val_raw[c], 0) for c in range(T // CHUNK)]
+        val_q = [quantize("val%d" % c, val_raw[c], 0) for c in range(3)]
+        neg_max = sb.tile([P, 1], F32, name="neg_max", tag="val2_grouped", align_bytes=64)
+        nc.vector.tensor_reduce(out=neg_max[:], in_=s[:], axis=mybir.AxisListType.X, op=ALU.max, negate=True)
+        val_q.append(quantize("val3", val_raw[3], 0))
 
         p = sb.tile([P, T], F32, name="p", tag="val3_raw")
         z = column("z")
         nc.scalar.activation(out=p[:], in_=s[:], func=ACT.Exp, bias=neg_max[:], accum_out=z[:])
         s_listed = sb.tile([P, I], F32, name="s_listed")
-        nc.vector.scalar_tensor_tensor(out=s_listed[:], in0=gap[:], scalar=rest[:], in1=b_sb[:], op0=ALU.mult, op1=ALU.add)
+        nc.vector.scalar_tensor_tensor(out=s_listed[:], in0=gap[:], scalar=neg_share[:, 0:1], in1=a_listed[:], op0=ALU.mult, op1=ALU.add)
         p_listed = sb.tile([P, I], F32, name="p_listed")
         nc.scalar.activation(out=p_listed[:], in_=s_listed[:], func=ACT.Exp, bias=neg_max[:])
 
-        neg_g = sb.tile([P, T], F32, name="neg_g")
-        for h in range(2):
-            bank = ps.tile([P, BANK], F32, name="c0_bank%d" % h, tag="late%d" % h)
-            for c in range(2):
-                codes, scales = val_q[2 * h + c]
-                nc.tensor.matmul_mx(out=bank[:, c * CHUNK : (c + 1) * CHUNK], lhsT=gout_codes[:].bitcast(FP8X4), lhsT_scale=gout_scales[:], rhs=codes[:].bitcast(FP8X4), rhs_scale=scales[:], start=True, stop=True)
-            nc.vector.scalar_tensor_tensor(out=neg_g[:, h * BANK : (h + 1) * BANK], in0=bank[:], scalar=-1.0, in1=fac_rows[:, h * BANK : (h + 1) * BANK], op0=ALU.mult, op1=ALU.mult)
+        neg_g = sb.tile([P, T], F32, name="neg_g", tag="val3_grouped", align_bytes=64)
+        for chunks, tag in (((0, 1), "late0"), ((2,), "late1"), ((3,), "late2")):
+            bank = ps.tile([P, len(chunks) * CHUNK], F32, name="c0_" + tag, tag=tag)
+            for n, c in enumerate(chunks):
+                codes, scales = val_q[c]
+                nc.tensor.matmul_mx(out=bank[:, n * CHUNK : (n + 1) * CHUNK], lhsT=gout_codes[:].bitcast(FP8X4), lhsT_scale=gout_scales[:], rhs=codes[:].bitcast(FP8X4), rhs_scale=scales[:], start=True, stop=True)
+            cols = slice(chunks[0] * CHUNK, (chunks[-1] + 1) * CHUNK)
+            nc.vector.scalar_tensor_tensor(out=neg_g[:, cols], in0=bank[:], scalar=-1.0, in1=fac_rows[:, cols], op0=ALU.mult, op1=ALU.mult)
 
         inv_z = column("inv_z")
         nc.vector.reciprocal(out=inv_z[:], in_=z[:])
@@ -203,7 +196,10 @@ def tile_attend_hvrefined_b_kernel(tc, query, fquery, ckeys, fkeys_words, fkeys_
         xds = sb.tile([P, T], F32, name="xds")
         nc.vector.scalar_tensor_tensor(out=xds[:], in0=prob[:], scalar=neg_cov[:], in1=neg_y[:], op0=ALU.mult, op1=ALU.subtract)
         xddl = sb.tile([P, I], F32, name="xddl")
-        nc.vector.tensor_copy(xddl[:], xds[:].indirect(offsets[:]))
         result = sb.tile([P, I], F32, name="result")
-        nc.vector.scalar_tensor_tensor(out=result[:], in0=xddl[:], scalar=out_scale[:], in1=base_sb[:], op0=ALU.mult, op1=ALU.add)
+        halves = [slice(0, I // 2), slice(I // 2, I)]
+        for h in range(2):
+            nc.vector.tensor_copy(xddl[:, halves[h]], xds[:].indirect(offsets[:, 8 * h : 8 * h + 8]))
+        for h in range(2):
+            nc.vector.scalar_tensor_tensor(out=result[:, halves[h]], in0=xddl[:, halves[h]], scalar=out_scale[:], in1=base_sb[:, halves[h]], op0=ALU.mult, op1=ALU.add)
         nc.sync.dma_start(out=out, in_=result[:])

from contextlib import ExitStack

import concourse.mybir as mybir
from concourse.masks import make_identity

D, K, E, T, I, Q = 512, 1024, 512, 1024, 256, 128
FLOPS = 2 * Q * (D * T + 2 * K * I + E * T)

F32 = mybir.dt.float32
BF16 = mybir.dt.bfloat16
I32 = mybir.dt.int32
U32 = mybir.dt.uint32
U16 = mybir.dt.uint16
U8 = mybir.dt.uint8
FP8X4 = mybir.dt.float8_e4m3fn_x4
ALU = mybir.AluOpType
ACT = mybir.ActivationFunctionType

P = 128
PACK = 4
CHUNK = 256
BANK = 512
LAST_ON_VECTOR = 160


def tile_attend_hvrefined_b_kernel(tc, query, fquery, ckeys, fkeys_words, fkeys_scales, share, gout, vals, fac, dfquery, base, offs, out):
    nc = tc.nc
    with ExitStack() as ctx:
        sb = ctx.enter_context(tc.tile_pool(name="sb", bufs=1))
        ps = ctx.enter_context(tc.psum_pool(name="ps", bufs=1))

        def load_rows(name, rows):
            passes, width = rows.shape[0] // (P * PACK), rows.shape[1]
            raw = sb.tile([P, passes, PACK, width], F32, name=name + "_raw", tag=name + "_raw")
            nc.sync.dma_start(out=raw[:], in_=rows.rearrange("(g p j) w -> p g j w", p=P, j=PACK))
            return raw

        def interleave(on_vector, grouped, raw):
            dst = grouped.rearrange("p (c i) t -> p c t i", i=4)
            src = raw.rearrange("p t (c i) -> p c t i", i=4)
            if on_vector:
                nc.vector.tensor_copy(out=dst, in_=src)
            else:
                nc.scalar.activation(out=dst, in_=src, func=ACT.Copy)

        def quantize(name, raw, vector_columns):
            passes, width = raw.shape[1], raw.shape[3]
            grouped = sb.tile([P, passes, width, PACK], BF16, name=name + "_grouped", tag=name + "_grouped", align_bytes=64)
            for g in range(passes):
                if vector_columns < width:
                    interleave(False, grouped[:, g, vector_columns:, :], raw[:, g, :, vector_columns:])
                if vector_columns > 0:
                    interleave(True, grouped[:, g, :vector_columns, :], raw[:, g, :, :vector_columns])
            codes = sb.tile([P, passes * width], U32, name=name + "_codes", align_bytes=64)
            scales = sb.tile([P, passes * width], U8, name=name + "_scales", align_bytes=64)
            nc.vector.quantize_mx(out=codes[:].bitcast(FP8X4), scales=scales[:], in_=grouped[:].rearrange("p g w t -> p (g w t)"))
            return codes, scales

        def column(name):
            return sb.tile([P, 1], F32, name=name)

        key_scales = sb.tile([P, T], U8, name="key_scales")
        nc.gpsimd.memset(key_scales[:].bitcast(I32), 0)
        identity = sb.tile([P, P], F32, name="identity")
        make_identity(nc, identity[:])

        fac_cols = sb.tile([P, T // P], F32, name="fac_cols")
        nc.sync.dma_start(out=fac_cols[:], in_=fac.rearrange("o (p c) -> p (o c)", p=P))
        offsets = sb.tile([P, I // 16], U16, name="offsets")
        nc.sync.dma_start(offsets[:], offs)

        def load_words(g):
            words = sb.tile([P, T], I32, name="key_words%d" % g)
            nc.sync.dma_start(out=words[:], in_=fkeys_words[g].rearrange("p n t -> p (n t)").bitcast(I32))
            return words

        dfq_raw = load_rows("dfq", dfquery)
        key_words = [load_words(0)]
        for quad in range(4):
            nc.sync.dma_start(out=key_scales[32 * quad : 32 * quad + 8, :].bitcast(I32), in_=fkeys_scales[:, 4 * quad : 4 * quad + 4, :].bitcast(I32))
        key_words.append(load_words(1))
        share_col = column("share_col")
        nc.sync.dma_start(out=share_col[:], in_=share)
        q_raw = load_rows("q", query)
        ck_raw = [load_rows("ck%d" % c, ckeys[:, c * CHUNK : (c + 1) * CHUNK]) for c in range(T // CHUNK)]
        fq_raw = [load_rows("fq%d" % g, fquery[g * P * PACK : (g + 1) * P * PACK, :]) for g in range(2)]
        gout_raw = load_rows("gout", gout)
        val_raw = [load_rows("val%d" % c, vals[:, c * CHUNK : (c + 1) * CHUNK]) for c in range(T // CHUNK)]
        base_sb = sb.tile([P, I], F32, name="base_sb")
        nc.sync.dma_start(out=base_sb[:], in_=base)

        xs = sb.tile([P, T], F32, name="xs")
        nc.vector.memset(xs[:], 0.0)
        df1 = sb.tile([P, T], F32, name="df1")
        nc.vector.memset(df1[:], 0.0)

        fac_rows = sb.tile([P, T], F32, name="fac_rows")
        for h in range(2):
            bank = ps.tile([P, 4, P], F32, name="fac_bank%d" % h, tag="late%d" % h)
            for c in range(4):
                nc.tensor.transpose(bank[:, c, :], fac_cols[:, 4 * h + c : 4 * h + c + 1].to_broadcast([P, P]), identity[:])
            nc.scalar.copy(out=fac_rows[:].rearrange("p (n e) -> p n e", e=8)[:, :, 4 * h : 4 * h + 4], in_=bank[:].rearrange("p c n -> p n c"))
        neg_share = sb.tile([P, I], F32, name="neg_share")
        nc.vector.tensor_scalar(out=neg_share[:], in0=share_col[:].to_broadcast([P, I]), scalar1=-1.0, scalar2=None, op0=ALU.mult)
        out_scale = column("out_scale")
        nc.vector.tensor_scalar(out=out_scale[:], in0=share_col[:], scalar1=1024.0, scalar2=None, op0=ALU.mult)

        dfq_codes, dfq_scales = quantize("dfq", dfq_raw, 0)
        picked_words = []
        for g in range(2):
            picked = sb.tile([P, I], U32, name="picked_words%d" % g, align_bytes=64)
            nc.vector.tensor_copy(picked[:], key_words[g][:].bitcast(U32).indirect(offsets[:]))
            picked_words.append(picked)
        picked_scales = sb.tile([P, I], U8, name="picked_scales", align_bytes=64)
        nc.vector.tensor_copy(picked_scales[:], key_scales[:].indirect(offsets[:]))

        def fine_product(acc, by_pass):
            for g, (codes, scales) in enumerate(by_pass):
                nc.tensor.matmul_mx(
                    out=acc,
                    lhsT=codes.bitcast(FP8X4),
                    lhsT_scale=scales,
                    rhs=picked_words[g][:].bitcast(FP8X4),
                    rhs_scale=picked_scales[4 * g :, :],
                    start=(g == 0),
                    stop=(g == 1),
                )

        q_codes, q_scales = quantize("q", q_raw, Q)
        tb_bank = ps.tile([P, I], F32, name="tb_bank", tag="late1")
        fine_product(tb_bank[:], [(dfq_codes[:, g * Q : (g + 1) * Q], dfq_scales[:, g * Q : (g + 1) * Q]) for g in range(2)])
        xdl = sb.tile([P, I], F32, name="xdl")
        nc.vector.tensor_scalar(out=xdl[:], in0=tb_bank[:], scalar1=share_col[:], scalar2=None, op0=ALU.mult)
        nc.vector.tensor_copy(xs[:].indirect(offsets[:]), xdl[:])

        ck_on_vector = [0, 0, 0, LAST_ON_VECTOR]
        a_banks = [ps.tile([P, BANK], F32, name="a_bank01"), ps.tile([P, CHUNK], F32, name="a_bank2"), ps.tile([P, CHUNK], F32, name="a_bank3")]
        a_out = [a_banks[0][:, :CHUNK], a_banks[0][:, CHUNK:], a_banks[1][:], a_banks[2][:]]
        for c in range(T // CHUNK):
            codes, scales = quantize("ck%d" % c, ck_raw[c], ck_on_vector[c])
            nc.tensor.matmul_mx(out=a_out[c], lhsT=q_codes[:].bitcast(FP8X4), lhsT_scale=q_scales[:], rhs=codes[:].bitcast(FP8X4), rhs_scale=scales[:], start=True, stop=True)
        fq = [quantize("fq%d" % g, fq_raw[g], g * Q) for g in range(2)]
        b_bank = ps.tile([P, I], F32, name="b_bank")
        fine_product(b_bank[:], [(codes[:], scales[:]) for codes, scales in fq])
        a_sb = sb.tile([P, T], F32, name="a_sb", tag="fq0_raw")
        nc.scalar.copy(out=a_sb[:, :BANK], in_=a_banks[0][:])
        nc.scalar.copy(out=a_sb[:, BANK : BANK + CHUNK], in_=a_banks[1][:])
        nc.vector.tensor_copy(out=a_sb[:, BANK + CHUNK :], in_=a_banks[2][:])

        a_listed = sb.tile([P, I], F32, name="a_listed")
        nc.vector.tensor_copy(a_listed[:], a_sb[:].indirect(offsets[:]))
        gap = sb.tile([P, I], F32, name="gap")
        nc.vector.tensor_tensor(gap[:], a_listed[:], b_bank[:], ALU.subtract)
        nc.vector.tensor_tensor(df1[:].indirect(offsets[:]), gap[:], neg_share[:], ALU.mult)
        s = sb.tile([P, T], F32, name="s")
        nc.vector.tensor_tensor(s[:], a_sb[:], df1[:], ALU.add)
        gout_codes, gout_scales = quantize("gout", gout_raw, 0)
        val_q = [quantize("val%d" % c, val_raw[c], 0) for c in range(3)]
        neg_max = sb.tile([P, 1], F32, name="neg_max", tag="val2_grouped", align_bytes=64)
        nc.vector.tensor_reduce(out=neg_max[:], in_=s[:], axis=mybir.AxisListType.X, op=ALU.max, negate=True)
        val_q.append(quantize("val3", val_raw[3], 0))

        p = sb.tile([P, T], F32, name="p", tag="val3_raw")
        z = column("z")
        nc.scalar.activation(out=p[:], in_=s[:], func=ACT.Exp, bias=neg_max[:], accum_out=z[:])
        s_listed = sb.tile([P, I], F32, name="s_listed")
        nc.vector.scalar_tensor_tensor(out=s_listed[:], in0=gap[:], scalar=neg_share[:, 0:1], in1=a_listed[:], op0=ALU.mult, op1=ALU.add)
        p_listed = sb.tile([P, I], F32, name="p_listed")
        nc.scalar.activation(out=p_listed[:], in_=s_listed[:], func=ACT.Exp, bias=neg_max[:])

        neg_g = sb.tile([P, T], F32, name="neg_g", tag="val3_grouped", align_bytes=64)
        for chunks, tag in (((0, 1), "late0"), ((2,), "late1"), ((3,), "late2")):
            bank = ps.tile([P, len(chunks) * CHUNK], F32, name="c0_" + tag, tag=tag)
            for n, c in enumerate(chunks):
                codes, scales = val_q[c]
                nc.tensor.matmul_mx(out=bank[:, n * CHUNK : (n + 1) * CHUNK], lhsT=gout_codes[:].bitcast(FP8X4), lhsT_scale=gout_scales[:], rhs=codes[:].bitcast(FP8X4), rhs_scale=scales[:], start=True, stop=True)
            cols = slice(chunks[0] * CHUNK, (chunks[-1] + 1) * CHUNK)
            nc.vector.scalar_tensor_tensor(out=neg_g[:, cols], in0=bank[:], scalar=-1.0, in1=fac_rows[:, cols], op0=ALU.mult, op1=ALU.mult)

        inv_z = column("inv_z")
        nc.vector.reciprocal(out=inv_z[:], in_=z[:])
        prob = sb.tile([P, T], F32, name="prob")
        nc.scalar.activation(out=prob[:], in_=p[:], func=ACT.Copy, scale=inv_z[:])

        spent = sb.tile([P, T], F32, name="spent")
        neg_mean_g = column("neg_mean_g")
        nc.vector.scalar_tensor_tensor(out=spent[:], in0=p[:], scalar=inv_z[:], in1=neg_g[:], op0=ALU.mult, op1=ALU.mult, accum_out=neg_mean_g[:])
        spent_listed = sb.tile([P, I], F32, name="spent_listed")
        mean_xs = column("mean_xs")
        nc.vector.scalar_tensor_tensor(out=spent_listed[:], in0=p_listed[:], scalar=inv_z[:], in1=xdl[:], op0=ALU.mult, op1=ALU.mult, accum_out=mean_xs[:])
        neg_v = sb.tile([P, T], F32, name="neg_v")
        nc.vector.scalar_tensor_tensor(out=neg_v[:], in0=neg_g[:], scalar=neg_mean_g[:], in1=prob[:], op0=ALU.subtract, op1=ALU.mult)
        neg_y = sb.tile([P, T], F32, name="neg_y")
        neg_cov = column("neg_cov")
        nc.vector.scalar_tensor_tensor(out=neg_y[:], in0=xs[:], scalar=mean_xs[:], in1=neg_v[:], op0=ALU.subtract, op1=ALU.mult, accum_out=neg_cov[:])
        xds = sb.tile([P, T], F32, name="xds")
        nc.vector.scalar_tensor_tensor(out=xds[:], in0=prob[:], scalar=neg_cov[:], in1=neg_y[:], op0=ALU.mult, op1=ALU.subtract)
        xddl = sb.tile([P, I], F32, name="xddl")
        result = sb.tile([P, I], F32, name="result")
        halves = [slice(0, I // 2), slice(I // 2, I)]
        for h in range(2):
            nc.vector.tensor_copy(xddl[:, halves[h]], xds[:].indirect(offsets[:, 8 * h : 8 * h + 8]))
        for h in range(2):
            nc.vector.scalar_tensor_tensor(out=result[:, halves[h]], in0=xddl[:, halves[h]], scalar=out_scale[:], in1=base_sb[:, halves[h]], op0=ALU.mult, op1=ALU.add)
        nc.sync.dma_start(out=out, in_=result[:])
